import numpy as np
import ml_dtypes


def mxq(x, axis, fmt="e4m3"):
    dtype, down = {"e4m3": (ml_dtypes.float8_e4m3fn, 7), "e5m2": (ml_dtypes.float8_e5m2, 14)}[fmt]
    v = np.moveaxis(np.asarray(x, np.float32).astype(ml_dtypes.bfloat16).astype(np.float64), axis, -1)
    blocks = v.reshape(v.shape[:-1] + (-1, 32))
    amax = np.abs(blocks).max(-1, keepdims=True)
    byte = np.maximum(np.where(amax > 0, np.frexp(amax)[1] - 1 + 127, 0) - down, 1)
    scale = np.exp2(byte - 127.0)
    codes = (blocks / scale).astype(np.float32).astype(dtype).astype(np.float64)
    return np.moveaxis((codes * scale).reshape(v.shape), -1, axis)


WIDE = False


def mx_kscale(k):
    if not WIDE:
        return np.ones(k)
    levels = np.array([10, -10, 5, -5, 0])
    if k % 512:
        return np.exp2(np.random.permutation(np.resize(levels, k // 32))).repeat(32)
    a = np.empty((k // 512, 16))
    for p in range(k // 512):
        a[p, :8] = np.random.permutation(np.resize(levels, 8))
        for g in range(8):
            far = levels[np.abs(levels - a[p, g]) >= 10]
            a[p, g + 8] = far[np.random.randint(len(far))]
    return np.exp2(a.ravel()).repeat(32)


def f64(x):
    return np.asarray(x).astype(np.float64)


def striped(idx):
    return np.tile(idx.reshape(-1, 16).T, (8, 1)).astype(np.uint16)


def unstriped(offs):
    return offs[:16].T.reshape(-1).astype(np.int64)


def pack_weight(w):
    k, n = w.shape
    w = f64(np.asarray(w, np.float32).astype(ml_dtypes.bfloat16)).reshape(k // 32, 32, n)
    amax = np.abs(w).max(1)
    byte = np.clip(np.where(amax > 0, np.frexp(amax)[1] - 1 + 127 - 7, 1), 1, 254)
    scaled = (w * np.exp2(127.0 - byte)[:, None, :]).reshape(k, n).astype(np.float32)
    words = np.ascontiguousarray(scaled.reshape(k // 512, 128, 4, n).transpose(0, 1, 3, 2)).astype(ml_dtypes.float8_e4m3fn).view(np.uint8)
    return words, np.ascontiguousarray(byte.astype(np.uint8).reshape(k // 512, 16, n))


def unpack_weight(words, scales):
    g, p, n, _ = words.shape
    vals = np.ascontiguousarray(words).view(ml_dtypes.float8_e4m3fn).astype(np.float64) * np.repeat(np.exp2(scales.astype(np.float64) - 127.0), 8, axis=1)[..., None]
    return vals.transpose(0, 1, 3, 2).reshape(g * 512, n)


E2M1 = np.array([0.0, 0.5, 1.0, 1.5, 2.0, 3.0, 4.0, 6.0, -0.0, -0.5, -1.0, -1.5, -2.0, -3.0, -4.0, -6.0])


def pack_fp4(w):
    k, n = w.shape
    w = f64(np.asarray(w, np.float32).astype(ml_dtypes.bfloat16)).reshape(k // 32, 32, n)
    amax = np.abs(w).max(1)
    mant, ex = np.frexp(amax / 6.0)
    byte = np.clip(np.where(amax > 0, np.where(mant > 0.5, ex, ex - 1) + 127, 1), 1, 254)
    scaled = (w * np.exp2(127.0 - byte)[:, None, :]).reshape(k, n).astype(np.float32)
    c = np.ascontiguousarray(scaled.reshape(k // 512, 128, 4, n).transpose(0, 1, 3, 2)).astype(ml_dtypes.float4_e2m1fn).view(np.uint8) & 0xF
    words = (c[..., 0::2] | (c[..., 1::2] << 4)).reshape(k // 512, 128, 2 * n)
    return np.ascontiguousarray(words), np.ascontiguousarray(byte.astype(np.uint8).reshape(k // 512, 16, n))


def unpack_fp4(words, scales):
    g, _, n = scales.shape
    words = np.ascontiguousarray(words).reshape(g, 128, n, 2)
    nib = np.empty((g, 128, n, 4), np.uint8)
    nib[..., 0::2] = words & 0xF
    nib[..., 1::2] = words >> 4
    vals = E2M1[nib] * np.repeat(np.exp2(scales.astype(np.float64) - 127.0), 8, axis=1)[..., None]
    return vals.transpose(0, 1, 3, 2).reshape(g * 512, n)


def planes(y):
    n, m = y.shape
    v = y.astype(np.float32).astype(ml_dtypes.bfloat16).astype(np.float64).reshape(n // 32, 32, m)
    top = np.abs(v).max(1)
    byte = np.clip(np.where(top > 0, np.frexp(top)[1] - 1 + 127 - 7, 1), 1, 254)
    codes = (v * np.exp2(127.0 - byte)[:, None, :]).reshape(n, m).astype(np.float32).astype(ml_dtypes.float8_e4m3fn).view(np.uint8)
    words = codes.reshape(n // 512, 128, 4, m).transpose(0, 1, 3, 2)
    return np.ascontiguousarray(words), np.ascontiguousarray(byte.astype(np.uint8).reshape(n // 512, 16, m))


K, T, S, N, H, W, G = 512, 2048, 512, 512, 512, 256, 2048


def setup_inputs():
    n = np.random.standard_normal
    s = mx_kscale(K)[:, None]
    u = mx_kscale(H)
    packed_xT = pack_weight(n((K, T)) * s)
    packed_w1 = pack_fp4(n((K, H)) / np.sqrt(K) / s)
    packed_w2 = pack_fp4(n((H, N)) / np.sqrt(H) / u[:, None])
    perm = np.random.permutation(S)
    return {
        "x_words": packed_xT[0],
        "x_scales": packed_xT[1],
        "w1_words": packed_w1[0],
        "w1_scales": packed_w1[1],
        "gn": (np.random.uniform(0.5, 1.5, (H, 1)) * u[:, None]).astype(np.float32),
        "w2_words": packed_w2[0],
        "w2_scales": packed_w2[1],
        "tau": np.random.uniform(0.3, 0.9, (N, 1)).astype(np.float32),
        "offs": striped(np.random.permutation(T)[:S]),
        "n1": striped(perm[:W]),
        "n2": striped(perm[W:]),
        "n3": striped(np.random.randint(0, S, G)),
    }


def reference(x_words, x_scales, w1_words, w1_scales, gn, w2_words, w2_scales, tau, offs, n1, n2, n3):
    xq = unpack_weight(x_words, x_scales)[:, unstriped(offs)]
    y = unpack_fp4(w1_words, w1_scales).T @ xq
    pa = y[:, unstriped(n1)]
    pb = y[:, unstriped(n2)]
    rb = np.minimum(pa, pb)
    ra = np.maximum(pa, pb)
    ds = np.zeros((H, S))
    ds[:, unstriped(n1)] = ra
    dt = ds.copy()
    dt[:, unstriped(n2)] = rb
    z = f64(gn) * dt
    h = unpack_fp4(w2_words, w2_scales).T @ mxq(z, 0, "e4m3")
    top = h.max(axis=1, keepdims=True)
    ea = np.exp(f64(tau) * (h[:, unstriped(n3)] - top))
    ms = ea.reshape(N, S, 4).sum(axis=2)
    out_0 = (1.5 * h) / (ms + 0.5)
    return (out_0,) + planes(out_0)

@@ -1,0 +1,245 @@
+from contextlib import ExitStack
+
+import concourse.mybir as mybir
+
+K, T, S, N, H, W, G = 512, 2048, 512, 512, 512, 256, 2048
+FLOPS = 2 * K * H * S + 2 * H * N * S
+
+F32 = mybir.dt.float32
+BF16 = mybir.dt.bfloat16
+I32 = mybir.dt.int32
+U32 = mybir.dt.uint32
+U16 = mybir.dt.uint16
+U8 = mybir.dt.uint8
+FP8X4 = mybir.dt.float8_e4m3fn_x4
+FP4X4 = mybir.dt.float4_e2m1fn_x4
+ALU = mybir.AluOpType
+ACT = mybir.ActivationFunctionType
+
+P = 128
+PACK = 4
+MEMBERS = 4
+LANES = 16
+PIECE = 128
+UNITS = ((0, 0, 256), (0, 256, 512), (1, 0, 512), (2, 0, 512), (3, 0, 384), (3, 384, 512))
+PLANE_CHUNKS = ((0, 256), (256, 384), (384, 512))
+
+
+def load_scale_rows(queue, plane, rows, quadrants):
+    for q in quadrants:
+        queue.dma_start(out=plane.bitcast(I32)[32 * q : 32 * q + 4, :], in_=rows.bitcast(I32)[4 * q : 4 * q + 4, :])
+
+
+def tile_picked_layorderegs_none_po_kernel(
+    tc, x_words, x_scales, w1_words, w1_scales, gn, w2_words, w2_scales, tau, offs, n1, n2, n3, out_0, out_1, out_2
+):
+    nc = tc.nc
+    with ExitStack() as ctx:
+        keep = ctx.enter_context(tc.tile_pool(name="keep", bufs=1))
+        psum = ctx.enter_context(tc.psum_pool(name="psum", bufs=1))
+
+        def tile(name, shape, dtype):
+            return keep.tile(shape, dtype, name=name, align_bytes=64)
+
+        offs_sb = tile("offs_sb", [P, S // LANES], U16)
+        n1_sb = tile("n1_sb", [P, W // LANES], U16)
+        n2_sb = tile("n2_sb", [P, W // LANES], U16)
+        n3_sb = tile("n3_sb", [P, G // LANES], U16)
+        xw = tile("xw", [P, T], I32)
+        xs = tile("xs", [P, T], U8)
+        w1w_raw = tile("w1w_raw", [P, 2 * H], U8)
+        w2w_raw = tile("w2w_raw", [P, 2 * N], U8)
+        w1s_raw = tile("w1s_raw", [P, H], U8)
+        w2s_raw = tile("w2s_raw", [P, N], U8)
+        gn_sb = tile("gn_sb", [P, PACK], F32)
+        tau_sb = tile("tau_sb", [P, PACK], F32)
+
+        nc.vector.memset(xs[:].bitcast(I32), 0)
+        nc.vector.memset(w1s_raw[:].bitcast(I32), 0)
+        nc.vector.memset(w2s_raw[:].bitcast(I32), 0)
+
+        nc.sync.dma_start(offs_sb[:], offs)
+        nc.sync.dma_start(out=xw[:], in_=x_words[0].rearrange("p n t -> p (n t)").bitcast(I32))
+        load_scale_rows(nc.scalar, xs[:], x_scales[0], range(4))
+        load_scale_rows(nc.scalar, w1s_raw[:], w1_scales[0], range(2))
+        load_scale_rows(nc.gpsimd, w1s_raw[:], w1_scales[0], range(2, 4))
+        nc.sync.dma_start(out=w1w_raw[:].bitcast(I32), in_=w1_words[0].bitcast(I32))
+        nc.sync.dma_start(n1_sb[:], n1)
+        nc.sync.dma_start(n2_sb[:], n2)
+        load_scale_rows(nc.sync, w2s_raw[:], w2_scales[0], range(4))
+        nc.sync.dma_start(out=w2w_raw[:].bitcast(I32), in_=w2_words[0].bitcast(I32))
+        nc.sync.dma_start(out=gn_sb[:], in_=gn.rearrange("(p t) o -> p (t o)", t=PACK))
+        nc.sync.dma_start(out=tau_sb[:], in_=tau.rearrange("(p t) o -> p (t o)", t=PACK))
+        nc.sync.dma_start(n3_sb[:], n3)
+
+        def deal(engine_copy, dealt, raw):
+            engine_copy(out=dealt.rearrange("p (t m) -> p t m", t=PACK), in_=raw.rearrange("p (m t) -> p t m", t=PACK))
+
+        w1w = tile("w1w", [P, 2 * H], U8)
+        w1s = tile("w1s", [P, H], U8)
+        w2w = tile("w2w", [P, 2 * N], U8)
+        w2s = tile("w2s", [P, N], U8)
+        deal(nc.scalar.copy, w1w[:].bitcast(U16), w1w_raw[:].bitcast(U16))
+        xw_pick = tile("xw_pick", [P, S], U32)
+        xs_pick = tile("xs_pick", [P, S], U8)
+        nc.vector.tensor_copy(xs_pick[:], xs[:].indirect(offs_sb[:]))
+        deal(nc.vector.tensor_copy, w1s[:], w1s_raw[:])
+        nc.vector.tensor_copy(xw_pick[:], xw[:].bitcast(U32).indirect(offs_sb[:]))
+        deal(nc.scalar.copy, w2w[:].bitcast(U16), w2w_raw[:].bitcast(U16))
+
+        def product(name, words, scales, codes, code_scales):
+            banks = []
+            for t in range(PACK):
+                bank = psum.tile([P, S], F32, name=f"{name}{t}")
+                nc.tensor.matmul_mx(
+                    out=bank[:],
+                    lhsT=words[:, 2 * P * t : 2 * P * (t + 1)].bitcast(FP4X4),
+                    lhsT_scale=scales[:, P * t : P * (t + 1)],
+                    rhs=codes.bitcast(FP8X4),
+                    rhs_scale=code_scales,
+                    start=True,
+                    stop=True,
+                )
+                banks.append(bank)
+            return banks
+
+        y_banks = product("y_bank", w1w, w1s, xw_pick[:], xs_pick[:])
+        deal(nc.vector.tensor_copy, w2s[:], w2s_raw[:])
+
+        rows = [tile(f"rows{t}", [P, 2 * S], F32) for t in range(PACK)]
+        y = [rows[t][:, S:] for t in range(PACK)]
+        h = [rows[t][:, :S] for t in range(PACK)]
+        pa = [tile(f"pa{t}", [P, W], F32) for t in range(PACK)]
+        pb = [tile(f"pb{t}", [P, W], F32) for t in range(PACK)]
+        ra = [tile(f"ra{t}", [P, W], F32) for t in range(PACK)]
+        rb = [tile(f"rb{t}", [P, W], F32) for t in range(PACK)]
+        dt = [tile(f"dt{t}", [P, S], F32) for t in range(PACK)]
+        z_bf = tile("z_bf", [P, S, PACK], BF16)
+
+        def scalar_move(out, in_):
+            nc.scalar.activation(out, in_, ACT.Copy)
+
+        def fetch(t, plain, move):
+            plain(y[t], y_banks[t][:])
+            move(pa[t][:], y[t].indirect(n1_sb[:]))
+            move(pb[t][:], y[t].indirect(n2_sb[:]))
+
+        def order(t):
+            nc.vector.tensor_tensor(ra[t][:], pa[t][:], pb[t][:], ALU.max)
+            nc.vector.tensor_tensor(rb[t][:], pa[t][:], pb[t][:], ALU.min)
+
+        def put_larger(t, move):
+            move(dt[t][:].indirect(n1_sb[:]), ra[t][:])
+
+        def put_smaller(t, move):
+            move(dt[t][:].indirect(n2_sb[:]), rb[t][:])
+
+        def gain(t):
+            nc.vector.tensor_scalar(z_bf[:, :, t], dt[t][:], gn_sb[:, t : t + 1], None, ALU.mult)
+
+        vector_move = nc.vector.tensor_copy
+        fetch(0, nc.scalar.copy, scalar_move)
+        fetch(1, vector_move, vector_move)
+        fetch(2, nc.scalar.copy, scalar_move)
+        fetch(3, nc.scalar.copy, scalar_move)
+        for t in range(PACK):
+            order(t)
+        for t in range(PACK):
+            move = scalar_move if t < 2 else vector_move
+            put_larger(t, move)
+            put_smaller(t, move)
+        for t in (2, 0, 3, 1):
+            gain(t)
+
+        z_codes = tile("z_codes", [P, S], U32)
+        z_scales = tile("z_scales", [P, S], U8)
+        nc.vector.quantize_mx(
+            out=z_codes[:].bitcast(FP8X4), scales=z_scales[:], in_=z_bf[:].rearrange("p c t -> p (c t)")
+        )
+        h_banks = product("h_bank", w2w, w2s, z_codes[:], z_scales[:])
+
+        top = [tile(f"top{t}", [P, 1], F32) for t in range(PACK)]
+        shift = [tile(f"shift{t}", [P, 1], F32) for t in range(PACK)]
+        for t in range(PACK):
+            nc.vector.tensor_scalar(h[t], h_banks[t][:], 1.0, None, ALU.mult, ALU.max, accum_out=top[t][:])
+            nc.vector.tensor_scalar(shift[t][:], top[t][:], tau_sb[:, t : t + 1], -1.0, ALU.mult, ALU.mult)
+
+        ea = [tile(f"ea{t}", [P, S, MEMBERS], F32) for t in range(PACK)]
+        for t in range(PACK):
+            for c in range(0, S, PIECE):
+                nc.scalar.activation(
+                    ea[t][:, c : c + PIECE, :].rearrange("p c e -> p (c e)"),
+                    rows[t][:].indirect(n3_sb[:, c * MEMBERS // LANES : (c + PIECE) * MEMBERS // LANES]),
+                    ACT.Exp,
+                    bias=shift[t][:],
+                    scale=tau_sb[:, t : t + 1],
+                )
+
+        out_rows = out_0.rearrange("(p t) c -> p t c", t=PACK)
+        res = tile("res", [P, PACK, S], F32)
+        half = [tile(f"half{i}", [P, hi - lo, 2], F32) for i, (t, lo, hi) in enumerate(UNITS)]
+        den = [tile(f"den{i}", [P, hi - lo], F32) for i, (t, lo, hi) in enumerate(UNITS)]
+
+        def add_halves(i):
+            t, lo, hi = UNITS[i]
+            nc.vector.tensor_tensor(half[i][:], ea[t][:, lo:hi, 0:2], ea[t][:, lo:hi, 2:4], ALU.add)
+
+        def add_up(i):
+            nc.vector.scalar_tensor_tensor(den[i][:], half[i][:, :, 0], 0.5, half[i][:, :, 1], ALU.add, ALU.add)
+
+        add_halves(0)
+        add_up(0)
+        for i, (t, lo, hi) in enumerate(UNITS):
+            quarter = (hi - lo) // 4
+            pair = tile(f"pair{i}", [P, 2, quarter], F32)
+            whole = tile(f"whole{i}", [P, quarter], F32)
+            inv = tile(f"inv{i}", [P, quarter], F32)
+            inv_pair = tile(f"inv_pair{i}", [P, 2, quarter], F32)
+            num = tile(f"num{i}", [P, 2, 2 * quarter], F32)
+            den_halves = den[i][:].rearrange("p (u c) -> p u c", u=2)
+            nc.vector.tensor_tensor(
+                pair[:].rearrange("p v c -> p (v c)"), den_halves[:, 0, :], den_halves[:, 1, :], ALU.mult
+            )
+            nc.vector.scalar_tensor_tensor(
+                num[:],
+                h[t][:, lo:hi].rearrange("p (u c) -> p u c", u=2),
+                1.5,
+                den_halves[:, ::-1, :],
+                ALU.mult,
+                ALU.mult,
+            )
+            nc.vector.tensor_tensor(whole[:], pair[:, 0, :], pair[:, 1, :], ALU.mult)
+            if i + 1 < len(UNITS):
+                add_halves(i + 1)
+            nc.vector.reciprocal(inv[:], whole[:])
+            if i + 1 < len(UNITS):
+                add_up(i + 1)
+            nc.vector.tensor_tensor(
+                inv_pair[:], inv[:].unsqueeze(1).to_broadcast([P, 2, quarter]), pair[:, ::-1, :], ALU.mult
+            )
+            nc.vector.tensor_tensor(
+                res[:, t, lo:hi].rearrange("p (u c) -> p u c", u=2),
+                num[:],
+                inv_pair[:].rearrange("p v c -> p (v c)").unsqueeze(1).to_broadcast([P, 2, 2 * quarter]),
+                ALU.mult,
+            )
+            nc.sync.dma_start(out=out_rows[:, t, lo:hi], in_=res[:, t, lo:hi])
+
+        res_bf = tile("res_bf", [P, S, PACK], BF16)
+        res_codes = tile("res_codes", [P, S], I32)
+        res_scales = tile("res_scales", [P, S], U8)
+        words_out = out_1[0].rearrange("p n t -> p (n t)").bitcast(I32)
+        for lo, hi in PLANE_CHUNKS:
+            nc.scalar.copy(out=res_bf[:, lo:hi, :], in_=res[:, :, lo:hi].rearrange("p t c -> p c t"))
+        for lo, hi in PLANE_CHUNKS:
+            nc.vector.quantize_mx(
+                out=res_codes[:, lo:hi].bitcast(FP8X4),
+                scales=res_scales[:, lo:hi],
+                in_=res_bf[:, lo:hi, :].rearrange("p c t -> p (c t)"),
+            )
+        nc.sync.dma_start(out=words_out, in_=res_codes[:])
+        for q in range(4):
+            queue = nc.scalar if q % 2 else nc.sync
+            queue.dma_start(
+                out=out_2[0].bitcast(I32)[4 * q : 4 * q + 4, :], in_=res_scales[:].bitcast(I32)[32 * q : 32 * q + 4, :]
+            )

@@ -1,6 +1,7 @@
 from contextlib import ExitStack
 
 import concourse.mybir as mybir
+from concourse.masks import make_identity
 
 K, T, S, N, H, W, G = 512, 2048, 512, 512, 512, 256, 2048
 FLOPS = 2 * K * H * S + 2 * H * N * S
@@ -21,8 +22,8 @@ PACK = 4
 MEMBERS = 4
 LANES = 16
 PIECE = 128
-UNITS = ((0, 0, 256), (0, 256, 512), (1, 0, 512), (2, 0, 512), (3, 0, 384), (3, 384, 512))
-PLANE_CHUNKS = ((0, 256), (256, 384), (384, 512))
+VECTOR_UNITS = (0, 7)
+HALF = S // 2
 
 
 def load_scale_rows(queue, plane, rows, quadrants):
@@ -38,8 +39,8 @@ def tile_picked_layorderegs_none_po_kernel(
         keep = ctx.enter_context(tc.tile_pool(name="keep", bufs=1))
         psum = ctx.enter_context(tc.psum_pool(name="psum", bufs=1))
 
-        def tile(name, shape, dtype):
-            return keep.tile(shape, dtype, name=name, align_bytes=64)
+        def tile(name, shape, dtype, tag=""):
+            return keep.tile(shape, dtype, name=name, tag=tag or name, align_bytes=64)
 
         offs_sb = tile("offs_sb", [P, S // LANES], U16)
         n1_sb = tile("n1_sb", [P, W // LANES], U16)
@@ -78,33 +79,36 @@ def tile_picked_layorderegs_none_po_kernel(
         w1w = tile("w1w", [P, 2 * H], U8)
         w1s = tile("w1s", [P, H], U8)
         w2w = tile("w2w", [P, 2 * N], U8)
-        w2s = tile("w2s", [P, N], U8)
         deal(nc.scalar.copy, w1w[:].bitcast(U16), w1w_raw[:].bitcast(U16))
         xw_pick = tile("xw_pick", [P, S], U32)
         xs_pick = tile("xs_pick", [P, S], U8)
         nc.vector.tensor_copy(xs_pick[:], xs[:].indirect(offs_sb[:]))
-        deal(nc.vector.tensor_copy, w1s[:], w1s_raw[:])
-        nc.vector.tensor_copy(xw_pick[:], xw[:].bitcast(U32).indirect(offs_sb[:]))
+        deal(nc.gpsimd.tensor_copy, w1s[:], w1s_raw[:])
+        for lo in (0, HALF):
+            entries = offs_sb[:, lo // LANES : (lo + HALF) // LANES]
+            nc.vector.tensor_copy(xw_pick[:, lo : lo + HALF], xw[:].bitcast(U32).indirect(entries))
         deal(nc.scalar.copy, w2w[:].bitcast(U16), w2w_raw[:].bitcast(U16))
 
         def product(name, words, scales, codes, code_scales):
-            banks = []
+            banks = [psum.tile([P, S], F32, name=f"{name}{t}") for t in range(PACK)]
             for t in range(PACK):
-                bank = psum.tile([P, S], F32, name=f"{name}{t}")
-                nc.tensor.matmul_mx(
-                    out=bank[:],
-                    lhsT=words[:, 2 * P * t : 2 * P * (t + 1)].bitcast(FP4X4),
-                    lhsT_scale=scales[:, P * t : P * (t + 1)],
-                    rhs=codes.bitcast(FP8X4),
-                    rhs_scale=code_scales,
-                    start=True,
-                    stop=True,
-                )
-                banks.append(bank)
+                for lo in (0, HALF):
+                    nc.tensor.matmul_mx(
+                        out=banks[t][:, lo : lo + HALF],
+                        lhsT=words[:, 2 * P * t : 2 * P * (t + 1)].bitcast(FP4X4),
+                        lhsT_scale=scales[:, P * t : P * (t + 1)],
+                        rhs=codes[:, lo : lo + HALF].bitcast(FP8X4),
+                        rhs_scale=code_scales[:, lo : lo + HALF],
+                        start=True,
+                        stop=True,
+                    )
             return banks
 
-        y_banks = product("y_bank", w1w, w1s, xw_pick[:], xs_pick[:])
-        deal(nc.vector.tensor_copy, w2s[:], w2s_raw[:])
+        y_banks = product("y_bank", w1w, w1s, xw_pick, xs_pick)
+        w2s = tile("w2s", [P, N], U8, tag="w1s_raw")
+        deal(nc.gpsimd.tensor_copy, w2s[:], w2s_raw[:])
+        ident = tile("ident", [P, P], F32, tag="w2s_raw")
+        make_identity(nc, ident[:])
 
         rows = [tile(f"rows{t}", [P, 2 * S], F32) for t in range(PACK)]
         y = [rows[t][:, S:] for t in range(PACK)]
@@ -114,15 +118,16 @@ def tile_picked_layorderegs_none_po_kernel(
         ra = [tile(f"ra{t}", [P, W], F32) for t in range(PACK)]
         rb = [tile(f"rb{t}", [P, W], F32) for t in range(PACK)]
         dt = [tile(f"dt{t}", [P, S], F32) for t in range(PACK)]
+        z_pairs = tile("z_pairs", [P, 2, S, 2], BF16)
         z_bf = tile("z_bf", [P, S, PACK], BF16)
 
         def scalar_move(out, in_):
             nc.scalar.activation(out, in_, ACT.Copy)
 
-        def fetch(t, plain, move):
+        def fetch(t, plain, move_a, move_b):
             plain(y[t], y_banks[t][:])
-            move(pa[t][:], y[t].indirect(n1_sb[:]))
-            move(pb[t][:], y[t].indirect(n2_sb[:]))
+            move_a(pa[t][:], y[t].indirect(n1_sb[:]))
+            move_b(pb[t][:], y[t].indirect(n2_sb[:]))
 
         def order(t):
             nc.vector.tensor_tensor(ra[t][:], pa[t][:], pb[t][:], ALU.max)
@@ -135,13 +140,14 @@ def tile_picked_layorderegs_none_po_kernel(
             move(dt[t][:].indirect(n2_sb[:]), rb[t][:])
 
         def gain(t):
-            nc.vector.tensor_scalar(z_bf[:, :, t], dt[t][:], gn_sb[:, t : t + 1], None, ALU.mult)
+            engine = nc.gpsimd if t < 2 else nc.vector
+            engine.tensor_scalar(z_pairs[:, t // 2, :, t % 2], dt[t][:], gn_sb[:, t : t + 1], 0.0, ALU.mult, ALU.add)
 
         vector_move = nc.vector.tensor_copy
-        fetch(0, nc.scalar.copy, scalar_move)
-        fetch(1, vector_move, vector_move)
-        fetch(2, nc.scalar.copy, scalar_move)
-        fetch(3, nc.scalar.copy, scalar_move)
+        fetch(0, nc.scalar.copy, scalar_move, scalar_move)
+        fetch(1, vector_move, vector_move, vector_move)
+        fetch(2, nc.scalar.copy, scalar_move, scalar_move)
+        fetch(3, nc.scalar.copy, scalar_move, vector_move)
         for t in range(PACK):
             order(t)
         for t in range(PACK):
@@ -153,10 +159,17 @@ def tile_picked_layorderegs_none_po_kernel(
 
         z_codes = tile("z_codes", [P, S], U32)
         z_scales = tile("z_scales", [P, S], U8)
-        nc.vector.quantize_mx(
-            out=z_codes[:].bitcast(FP8X4), scales=z_scales[:], in_=z_bf[:].rearrange("p c t -> p (c t)")
-        )
-        h_banks = product("h_bank", w2w, w2s, z_codes[:], z_scales[:])
+        pair_words = z_pairs[:].rearrange("p u c e -> p u (c e)").bitcast(F32).rearrange("p u c -> p c u")
+        z_words = z_bf[:].rearrange("p c t -> p (c t)").bitcast(F32).rearrange("p (c u) -> p c u", u=2)
+        for lo in (0, HALF):
+            nc.vector.tensor_copy(z_words[:, lo : lo + HALF, :], pair_words[:, lo : lo + HALF, :])
+        for lo in (0, HALF):
+            nc.vector.quantize_mx(
+                out=z_codes[:, lo : lo + HALF].bitcast(FP8X4),
+                scales=z_scales[:, lo : lo + HALF],
+                in_=z_bf[:, lo : lo + HALF, :].rearrange("p c t -> p (c t)"),
+            )
+        h_banks = product("h_bank", w2w, w2s, z_codes, z_scales)
 
         top = [tile(f"top{t}", [P, 1], F32) for t in range(PACK)]
         shift = [tile(f"shift{t}", [P, 1], F32) for t in range(PACK)]
@@ -164,80 +177,141 @@ def tile_picked_layorderegs_none_po_kernel(
             nc.vector.tensor_scalar(h[t], h_banks[t][:], 1.0, None, ALU.mult, ALU.max, accum_out=top[t][:])
             nc.vector.tensor_scalar(shift[t][:], top[t][:], tau_sb[:, t : t + 1], -1.0, ALU.mult, ALU.mult)
 
-        ea = [tile(f"ea{t}", [P, S, MEMBERS], F32) for t in range(PACK)]
-        for t in range(PACK):
-            for c in range(0, S, PIECE):
+        out_rows = out_0.rearrange("(p t) c -> p t c", t=PACK)
+        res = tile("res", [P, PACK * S], F32)
+
+        mid, quarter = HALF // 2, HALF // 4
+
+        def steps(i):
+            t, lo = i % PACK, i // PACK * HALF
+            first = t * S + lo
+            ea = tile(f"ea{i}", [P, HALF * MEMBERS], F32)
+            for c in range(0, HALF, PIECE):
                 nc.scalar.activation(
-                    ea[t][:, c : c + PIECE, :].rearrange("p c e -> p (c e)"),
-                    rows[t][:].indirect(n3_sb[:, c * MEMBERS // LANES : (c + PIECE) * MEMBERS // LANES]),
+                    ea[:, c * MEMBERS : (c + PIECE) * MEMBERS],
+                    rows[t][:].indirect(n3_sb[:, (lo + c) * MEMBERS // LANES : (lo + c + PIECE) * MEMBERS // LANES]),
                     ACT.Exp,
                     bias=shift[t][:],
                     scale=tau_sb[:, t : t + 1],
                 )
-
-        out_rows = out_0.rearrange("(p t) c -> p t c", t=PACK)
-        res = tile("res", [P, PACK, S], F32)
-        half = [tile(f"half{i}", [P, hi - lo, 2], F32) for i, (t, lo, hi) in enumerate(UNITS)]
-        den = [tile(f"den{i}", [P, hi - lo], F32) for i, (t, lo, hi) in enumerate(UNITS)]
-
-        def add_halves(i):
-            t, lo, hi = UNITS[i]
-            nc.vector.tensor_tensor(half[i][:], ea[t][:, lo:hi, 0:2], ea[t][:, lo:hi, 2:4], ALU.add)
-
-        def add_up(i):
-            nc.vector.scalar_tensor_tensor(den[i][:], half[i][:, :, 0], 0.5, half[i][:, :, 1], ALU.add, ALU.add)
-
-        add_halves(0)
-        add_up(0)
-        for i, (t, lo, hi) in enumerate(UNITS):
-            quarter = (hi - lo) // 4
             pair = tile(f"pair{i}", [P, 2, quarter], F32)
+            pair_flat = pair[:].rearrange("p v c -> p (v c)")
             whole = tile(f"whole{i}", [P, quarter], F32)
             inv = tile(f"inv{i}", [P, quarter], F32)
             inv_pair = tile(f"inv_pair{i}", [P, 2, quarter], F32)
-            num = tile(f"num{i}", [P, 2, 2 * quarter], F32)
-            den_halves = den[i][:].rearrange("p (u c) -> p u c", u=2)
-            nc.vector.tensor_tensor(
-                pair[:].rearrange("p v c -> p (v c)"), den_halves[:, 0, :], den_halves[:, 1, :], ALU.mult
-            )
-            nc.vector.scalar_tensor_tensor(
-                num[:],
-                h[t][:, lo:hi].rearrange("p (u c) -> p u c", u=2),
-                1.5,
-                den_halves[:, ::-1, :],
-                ALU.mult,
-                ALU.mult,
-            )
-            nc.vector.tensor_tensor(whole[:], pair[:, 0, :], pair[:, 1, :], ALU.mult)
-            if i + 1 < len(UNITS):
-                add_halves(i + 1)
-            nc.vector.reciprocal(inv[:], whole[:])
-            if i + 1 < len(UNITS):
-                add_up(i + 1)
-            nc.vector.tensor_tensor(
-                inv_pair[:], inv[:].unsqueeze(1).to_broadcast([P, 2, quarter]), pair[:, ::-1, :], ALU.mult
-            )
-            nc.vector.tensor_tensor(
-                res[:, t, lo:hi].rearrange("p (u c) -> p u c", u=2),
-                num[:],
-                inv_pair[:].rearrange("p v c -> p (v c)").unsqueeze(1).to_broadcast([P, 2, 2 * quarter]),
-                ALU.mult,
-            )
-            nc.sync.dma_start(out=out_rows[:, t, lo:hi], in_=res[:, t, lo:hi])
+            inv_flat = inv_pair[:].rearrange("p v c -> p (v c)")
+            members = ea[:].rearrange("p (c e) -> p c e", e=MEMBERS)
 
-        res_bf = tile("res_bf", [P, S, PACK], BF16)
-        res_codes = tile("res_codes", [P, S], I32)
+            def join():
+                nc.vector.tensor_tensor(whole[:], pair[:, 0, :], pair[:, 1, :], ALU.mult)
+
+            def invert():
+                nc.vector.reciprocal(inv[:], whole[:])
+
+            def spread():
+                nc.vector.tensor_tensor(
+                    inv_pair[:], inv[:].unsqueeze(1).to_broadcast([P, 2, quarter]), pair[:, ::-1, :], ALU.mult
+                )
+
+            def store():
+                nc.sync.dma_start(out=out_rows[:, t, lo : lo + HALF], in_=res[:, first : first + HALF])
+
+            if i in VECTOR_UNITS:
+                half = tile(f"half{i}", [P, HALF, 2], F32, tag=f"whole{i - 1}")
+                den = tile(f"den{i}", [P, HALF], F32)
+                num = tile(f"num{i}", [P, HALF], F32)
+
+                def add_halves():
+                    nc.vector.tensor_tensor(half[:], members[:, :, 0:2], members[:, :, 2:4], ALU.add)
+
+                def add_up():
+                    nc.vector.scalar_tensor_tensor(den[:], half[:, :, 0], 0.5, half[:, :, 1], ALU.add, ALU.add)
+
+                def pair_up():
+                    nc.vector.tensor_tensor(pair_flat, den[:, :mid], den[:, mid:], ALU.mult)
+
+                def numerator():
+                    nc.vector.scalar_tensor_tensor(
+                        num[:].rearrange("p (u c) -> p u c", u=2),
+                        h[t][:, lo : lo + HALF].rearrange("p (u c) -> p u c", u=2),
+                        1.5,
+                        den[:].rearrange("p (u c) -> p u c", u=2)[:, ::-1, :],
+                        ALU.mult,
+                        ALU.mult,
+                    )
+
+                def finish():
+                    nc.vector.tensor_tensor(
+                        res[:, first : first + HALF].rearrange("p (u c) -> p u c", u=2),
+                        num[:].rearrange("p (u c) -> p u c", u=2),
+                        inv_flat.unsqueeze(1).to_broadcast([P, 2, mid]),
+                        ALU.mult,
+                    )
+                    store()
+
+                return [add_halves, add_up, pair_up, numerator, join, invert], [spread, finish]
+
+            sums = y_banks[i % 2]
+            back = y_banks[2 + i % 2]
+            upper = tile(f"upper{i}", [P, mid], F32)
+            recip = tile(f"recip{i}", [P, HALF], F32)
+
+            def turn_and_add():
+                for u in range(2):
+                    for e in range(MEMBERS):
+                        nc.tensor.matmul(
+                            sums[:, u * mid : (u + 1) * mid],
+                            members[:, u * mid : (u + 1) * mid, e],
+                            ident[:],
+                            is_transpose=True,
+                            start=(e == 0),
+                            stop=(e == MEMBERS - 1),
+                        )
+                nc.vector.tensor_scalar(upper[:], sums[:, mid:HALF], 0.5, None, ALU.add)
+
+            def pair_up():
+                nc.vector.scalar_tensor_tensor(pair_flat, sums[:, :mid], 0.5, upper[:], ALU.add, ALU.mult)
+
+            def split():
+                nc.vector.tensor_tensor(recip[:, :mid], upper[:], inv_flat, ALU.mult)
+                nc.vector.scalar_tensor_tensor(recip[:, mid:], sums[:, :mid], 0.5, inv_flat, ALU.add, ALU.mult)
+                for u in range(2):
+                    nc.tensor.transpose(back[:, u * mid : (u + 1) * mid], recip[:, u * mid : (u + 1) * mid], ident[:])
+
+            def finish():
+                nc.vector.scalar_tensor_tensor(
+                    res[:, first : first + HALF], h[t][:, lo : lo + HALF], 1.5, back[:, :HALF], ALU.mult, ALU.mult
+                )
+                store()
+
+            return [turn_and_add, pair_up, join, invert], [spread, split, finish]
+
+        late = []
+        for i in range(2 * PACK):
+            early, rest = steps(i)
+            for j in range(max(len(early), len(late))):
+                if j < len(early):
+                    early[j]()
+                if j < len(late):
+                    late[j]()
+            late = rest
+        for step in late:
+            step()
+
+        res_bf = [tile(f"res_bf{i}", [P, HALF, PACK], BF16, tag=f"shift{PACK - 1 - i}") for i in range(2)]
+        res_codes = tile("res_codes", [P, S], I32, tag=f"num{2 * PACK - 1}")
         res_scales = tile("res_scales", [P, S], U8)
         words_out = out_1[0].rearrange("p n t -> p (n t)").bitcast(I32)
-        for lo, hi in PLANE_CHUNKS:
-            nc.scalar.copy(out=res_bf[:, lo:hi, :], in_=res[:, :, lo:hi].rearrange("p t c -> p c t"))
-        for lo, hi in PLANE_CHUNKS:
+        res_cols = res[:].rearrange("p (t c) -> p c t", t=PACK)
+        for i, copy in enumerate((nc.scalar.copy, nc.vector.tensor_copy)):
+            cols = slice(i * HALF, (i + 1) * HALF)
+            copy(out=res_bf[i][:], in_=res_cols[:, cols, :])
             nc.vector.quantize_mx(
-                out=res_codes[:, lo:hi].bitcast(FP8X4),
-                scales=res_scales[:, lo:hi],
-                in_=res_bf[:, lo:hi, :].rearrange("p c t -> p (c t)"),
+                out=res_codes[:, cols].bitcast(FP8X4),
+                scales=res_scales[:, cols],
+                in_=res_bf[i][:].rearrange("p c t -> p (c t)"),
             )
-        nc.sync.dma_start(out=words_out, in_=res_codes[:])
+            nc.sync.dma_start(out=words_out[:, cols], in_=res_codes[:, cols])
         for q in range(4):
             queue = nc.scalar if q % 2 else nc.sync
             queue.dma_start(

@@ -22,7 +22,8 @@ PACK = 4
 MEMBERS = 4
 LANES = 16
 PIECE = 128
-VECTOR_UNITS = (0, 7)
+VECTOR_UNITS = (7,)
+SCALAR_LAST = 96
 HALF = S // 2
 
 
@@ -161,8 +162,8 @@ def tile_picked_layorderegs_none_po_kernel(
         z_scales = tile("z_scales", [P, S], U8)
         pair_words = z_pairs[:].rearrange("p u c e -> p u (c e)").bitcast(F32).rearrange("p u c -> p c u")
         z_words = z_bf[:].rearrange("p c t -> p (c t)").bitcast(F32).rearrange("p (c u) -> p c u", u=2)
-        for lo in (0, HALF):
-            nc.vector.tensor_copy(z_words[:, lo : lo + HALF, :], pair_words[:, lo : lo + HALF, :])
+        nc.vector.tensor_copy(z_words[:, :HALF, :], pair_words[:, :HALF, :])
+        nc.scalar.copy(z_words[:, HALF:, :], pair_words[:, HALF:, :])
         for lo in (0, HALF):
             nc.vector.quantize_mx(
                 out=z_codes[:, lo : lo + HALF].bitcast(FP8X4),
@@ -181,11 +182,12 @@ def tile_picked_layorderegs_none_po_kernel(
         res = tile("res", [P, PACK * S], F32)
 
         mid, quarter = HALF // 2, HALF // 4
+        units = [(i % PACK, i // PACK * HALF) for i in range(2 * PACK)]
 
-        def steps(i):
-            t, lo = i % PACK, i // PACK * HALF
-            first = t * S + lo
+        members = []
+        for i, (t, lo) in enumerate(units):
             ea = tile(f"ea{i}", [P, HALF * MEMBERS], F32)
+            members.append(ea[:].rearrange("p (c e) -> p c e", e=MEMBERS))
             for c in range(0, HALF, PIECE):
                 nc.scalar.activation(
                     ea[:, c * MEMBERS : (c + PIECE) * MEMBERS],
@@ -194,122 +196,121 @@ def tile_picked_layorderegs_none_po_kernel(
                     bias=shift[t][:],
                     scale=tau_sb[:, t : t + 1],
                 )
-            pair = tile(f"pair{i}", [P, 2, quarter], F32)
-            pair_flat = pair[:].rearrange("p v c -> p (v c)")
+
+        def parts(ap, count):
+            return ap.rearrange("p (v c) -> p v c", v=count)
+
+        def turn_and_add(i, u):
+            bank = y_banks[2 + i % 2 if u else 0][:, :mid]
+            for e in range(MEMBERS):
+                nc.tensor.matmul(
+                    bank,
+                    members[i][:, u * mid : (u + 1) * mid, e],
+                    ident[:],
+                    is_transpose=True,
+                    start=(e == 0),
+                    stop=(e == MEMBERS - 1),
+                )
+            return bank
+
+        def add_halves(i, half, u):
+            block = members[i][:, u * mid : (u + 1) * mid, :]
+            nc.vector.tensor_tensor(half[:, u, :, :], block[:, :, 0:2], block[:, :, 2:4], ALU.add)
+
+        def add_up(half, den, u):
+            nc.vector.scalar_tensor_tensor(den[:, u, :], half[:, u, :, 0], 0.5, half[:, u, :, 1], ALU.add, ALU.add)
+
+        def begin(i):
+            if i in VECTOR_UNITS:
+                half = tile(f"half{i}", [P, 2, mid, 2], F32, tag=f"whole{i - 1}")
+                add_halves(i, half, 0)
+                return half
+            early = tile(f"early{i}", [P, mid], F32, tag=f"whole{i - 1}")
+            nc.vector.tensor_scalar(early[:], turn_and_add(i, 0), 0.5, None, ALU.add)
+            return early
+
+        def store(i):
+            t, lo = units[i]
+            nc.sync.dma_start(out=out_rows[:, t, lo : lo + HALF], in_=res[:, t * S + lo : t * S + lo + HALF])
+
+        def finish(i):
+            if i < 0 or i in VECTOR_UNITS:
+                return
+            t, lo = units[i]
+            nc.vector.scalar_tensor_tensor(
+                res[:, t * S + lo : t * S + lo + HALF],
+                h[t][:, lo : lo + HALF],
+                1.5,
+                y_banks[2 + i % 2][:, mid : mid + HALF],
+                ALU.mult,
+                ALU.mult,
+            )
+            store(i)
+
+        begun = begin(0)
+        for i, (t, lo) in enumerate(units):
+            pair = tile(f"pair{i}", [P, mid], F32)
+            pair_swapped = parts(pair[:], 2)[:, ::-1, :]
             whole = tile(f"whole{i}", [P, quarter], F32)
             inv = tile(f"inv{i}", [P, quarter], F32)
-            inv_pair = tile(f"inv_pair{i}", [P, 2, quarter], F32)
-            inv_flat = inv_pair[:].rearrange("p v c -> p (v c)")
-            members = ea[:].rearrange("p (c e) -> p c e", e=MEMBERS)
-
-            def join():
-                nc.vector.tensor_tensor(whole[:], pair[:, 0, :], pair[:, 1, :], ALU.mult)
-
-            def invert():
-                nc.vector.reciprocal(inv[:], whole[:])
-
-            def spread():
-                nc.vector.tensor_tensor(
-                    inv_pair[:], inv[:].unsqueeze(1).to_broadcast([P, 2, quarter]), pair[:, ::-1, :], ALU.mult
-                )
-
-            def store():
-                nc.sync.dma_start(out=out_rows[:, t, lo : lo + HALF], in_=res[:, first : first + HALF])
-
+            inv_all = inv[:].unsqueeze(1).to_broadcast([P, 4, quarter])
+            others = tile(f"others{i}", [P, HALF], F32)
             if i in VECTOR_UNITS:
-                half = tile(f"half{i}", [P, HALF, 2], F32, tag=f"whole{i - 1}")
-                den = tile(f"den{i}", [P, HALF], F32)
+                den = tile(f"den{i}", [P, 2, mid], F32)
                 num = tile(f"num{i}", [P, HALF], F32)
-
-                def add_halves():
-                    nc.vector.tensor_tensor(half[:], members[:, :, 0:2], members[:, :, 2:4], ALU.add)
-
-                def add_up():
-                    nc.vector.scalar_tensor_tensor(den[:], half[:, :, 0], 0.5, half[:, :, 1], ALU.add, ALU.add)
-
-                def pair_up():
-                    nc.vector.tensor_tensor(pair_flat, den[:, :mid], den[:, mid:], ALU.mult)
-
-                def numerator():
-                    nc.vector.scalar_tensor_tensor(
-                        num[:].rearrange("p (u c) -> p u c", u=2),
-                        h[t][:, lo : lo + HALF].rearrange("p (u c) -> p u c", u=2),
-                        1.5,
-                        den[:].rearrange("p (u c) -> p u c", u=2)[:, ::-1, :],
-                        ALU.mult,
-                        ALU.mult,
-                    )
-
-                def finish():
-                    nc.vector.tensor_tensor(
-                        res[:, first : first + HALF].rearrange("p (u c) -> p u c", u=2),
-                        num[:].rearrange("p (u c) -> p u c", u=2),
-                        inv_flat.unsqueeze(1).to_broadcast([P, 2, mid]),
-                        ALU.mult,
-                    )
-                    store()
-
-                return [add_halves, add_up, pair_up, numerator, join, invert], [spread, finish]
-
-            sums = y_banks[i % 2]
-            back = y_banks[2 + i % 2]
-            upper = tile(f"upper{i}", [P, mid], F32)
-            recip = tile(f"recip{i}", [P, HALF], F32)
-
-            def turn_and_add():
-                for u in range(2):
-                    for e in range(MEMBERS):
-                        nc.tensor.matmul(
-                            sums[:, u * mid : (u + 1) * mid],
-                            members[:, u * mid : (u + 1) * mid, e],
-                            ident[:],
-                            is_transpose=True,
-                            start=(e == 0),
-                            stop=(e == MEMBERS - 1),
-                        )
-                nc.vector.tensor_scalar(upper[:], sums[:, mid:HALF], 0.5, None, ALU.add)
-
-            def pair_up():
-                nc.vector.scalar_tensor_tensor(pair_flat, sums[:, :mid], 0.5, upper[:], ALU.add, ALU.mult)
-
-            def split():
-                nc.vector.tensor_tensor(recip[:, :mid], upper[:], inv_flat, ALU.mult)
-                nc.vector.scalar_tensor_tensor(recip[:, mid:], sums[:, :mid], 0.5, inv_flat, ALU.add, ALU.mult)
-                for u in range(2):
-                    nc.tensor.transpose(back[:, u * mid : (u + 1) * mid], recip[:, u * mid : (u + 1) * mid], ident[:])
-
-            def finish():
+                add_up(begun, den, 0)
+                add_halves(i, begun, 1)
+                finish(i - 2)
+                add_up(begun, den, 1)
+                nc.vector.tensor_tensor(pair[:], den[:, 0, :], den[:, 1, :], ALU.mult)
                 nc.vector.scalar_tensor_tensor(
-                    res[:, first : first + HALF], h[t][:, lo : lo + HALF], 1.5, back[:, :HALF], ALU.mult, ALU.mult
+                    parts(num[:], 2), parts(h[t][:, lo : lo + HALF], 2), 1.5, den[:, ::-1, :], ALU.mult, ALU.mult
                 )
-                store()
+                nc.vector.tensor_tensor(whole[:], pair[:, :quarter], pair[:, quarter:], ALU.mult)
+                nc.vector.tensor_tensor(
+                    others[:].rearrange("p (u v c) -> p u v c", u=2, v=2),
+                    num[:].rearrange("p (u v c) -> p u v c", u=2, v=2),
+                    pair_swapped.unsqueeze(1).to_broadcast([P, 2, 2, quarter]),
+                    ALU.mult,
+                )
+                nc.vector.reciprocal(inv[:], whole[:])
+                if i + 1 < len(units):
+                    begun = begin(i + 1)
+                finish(i - 1)
+                nc.vector.tensor_tensor(
+                    parts(res[:, t * S + lo : t * S + lo + HALF], 4), parts(others[:], 4), inv_all, ALU.mult
+                )
+                store(i)
+                continue
+            early, late = begun, turn_and_add(i, 1)
+            recip = tile(f"recip{i}", [P, HALF], F32)
+            nc.vector.scalar_tensor_tensor(pair[:], late, 0.5, early[:], ALU.add, ALU.mult)
+            finish(i - 2)
+            nc.vector.tensor_tensor(whole[:], pair[:, :quarter], pair[:, quarter:], ALU.mult)
+            nc.gpsimd.tensor_tensor(parts(others[:, mid:], 2), parts(early[:], 2), pair_swapped, ALU.mult)
+            nc.vector.scalar_tensor_tensor(parts(others[:, :mid], 2), parts(late, 2), 0.5, pair_swapped, ALU.add, ALU.mult)
+            nc.vector.reciprocal(inv[:], whole[:])
+            nc.gpsimd.tensor_tensor(parts(recip[:], 4), parts(others[:], 4), inv_all, ALU.mult)
+            for u in range(2):
+                cols = slice(u * mid, (u + 1) * mid)
+                nc.tensor.transpose(y_banks[2 + i % 2][:, (u + 1) * mid : (u + 2) * mid], recip[:, cols], ident[:])
+            begun = begin(i + 1)
 
-            return [turn_and_add, pair_up, join, invert], [spread, split, finish]
-
-        late = []
-        for i in range(2 * PACK):
-            early, rest = steps(i)
-            for j in range(max(len(early), len(late))):
-                if j < len(early):
-                    early[j]()
-                if j < len(late):
-                    late[j]()
-            late = rest
-        for step in late:
-            step()
-
-        res_bf = [tile(f"res_bf{i}", [P, HALF, PACK], BF16, tag=f"shift{PACK - 1 - i}") for i in range(2)]
-        res_codes = tile("res_codes", [P, S], I32, tag=f"num{2 * PACK - 1}")
+        res_bf = tile("res_bf", [P, S, PACK], BF16, tag=f"shift{PACK - 1}")
+        res_codes = tile("res_codes", [P, S], I32, tag=f"inv{2 * PACK - 1}")
         res_scales = tile("res_scales", [P, S], U8)
         words_out = out_1[0].rearrange("p n t -> p (n t)").bitcast(I32)
         res_cols = res[:].rearrange("p (t c) -> p c t", t=PACK)
-        for i, copy in enumerate((nc.scalar.copy, nc.vector.tensor_copy)):
-            cols = slice(i * HALF, (i + 1) * HALF)
-            copy(out=res_bf[i][:], in_=res_cols[:, cols, :])
+        cut = HALF + SCALAR_LAST
+        nc.scalar.copy(out=res_bf[:, :HALF, :], in_=res_cols[:, :HALF, :])
+        nc.scalar.copy(out=res_bf[:, HALF:cut, :], in_=res_cols[:, HALF:cut, :])
+        nc.vector.tensor_copy(out=res_bf[:, cut:, :], in_=res_cols[:, cut:, :])
+        for lo in (0, HALF):
+            cols = slice(lo, lo + HALF)
             nc.vector.quantize_mx(
                 out=res_codes[:, cols].bitcast(FP8X4),
                 scales=res_scales[:, cols],
-                in_=res_bf[i][:].rearrange("p c t -> p (c t)"),
+                in_=res_bf[:, cols, :].rearrange("p c t -> p (c t)"),
             )
             nc.sync.dma_start(out=words_out[:, cols], in_=res_codes[:, cols])
         for q in range(4):

@@ -22,7 +22,7 @@ PACK = 4
 MEMBERS = 4
 LANES = 16
 PIECE = 128
-VECTOR_UNITS = (7,)
+VECTOR_UNITS = (3, 7)
 SCALAR_LAST = 96
 HALF = S // 2
 
@@ -290,11 +290,12 @@ def tile_picked_layorderegs_none_po_kernel(
             nc.gpsimd.tensor_tensor(parts(others[:, mid:], 2), parts(early[:], 2), pair_swapped, ALU.mult)
             nc.vector.scalar_tensor_tensor(parts(others[:, :mid], 2), parts(late, 2), 0.5, pair_swapped, ALU.add, ALU.mult)
             nc.vector.reciprocal(inv[:], whole[:])
-            nc.gpsimd.tensor_tensor(parts(recip[:], 4), parts(others[:], 4), inv_all, ALU.mult)
+            begun = begin(i + 1)
+            engine = nc.vector if i + 1 in VECTOR_UNITS else nc.gpsimd
+            engine.tensor_tensor(parts(recip[:], 4), parts(others[:], 4), inv_all, ALU.mult)
             for u in range(2):
                 cols = slice(u * mid, (u + 1) * mid)
                 nc.tensor.transpose(y_banks[2 + i % 2][:, (u + 1) * mid : (u + 2) * mid], recip[:, cols], ident[:])
-            begun = begin(i + 1)
 
         res_bf = tile("res_bf", [P, S, PACK], BF16, tag=f"shift{PACK - 1}")
         res_codes = tile("res_codes", [P, S], I32, tag=f"inv{2 * PACK - 1}")

@@ -19,17 +19,28 @@ ACT = mybir.ActivationFunctionType
 
 P = 128
 PACK = 4
+QUADRANTS = 4
 MEMBERS = 4
 LANES = 16
-PIECE = 128
-VECTOR_UNITS = (3, 7)
-SCALAR_LAST = 96
 HALF = S // 2
+BLOCK = P
+QUARTER = HALF // 4
+UNITS = tuple((t, lo) for lo in (0, HALF) for t in range(PACK))
+VECTOR_UNITS = (0, len(UNITS) - 1)
+SCALAR_LAST = 96
 
 
 def load_scale_rows(queue, plane, rows, quadrants):
     for q in quadrants:
         queue.dma_start(out=plane.bitcast(I32)[32 * q : 32 * q + 4, :], in_=rows.bitcast(I32)[4 * q : 4 * q + 4, :])
+
+
+def deal(copy, dealt, raw):
+    copy(out=dealt.rearrange("p (t m) -> p t m", t=PACK), in_=raw.rearrange("p (m t) -> p t m", t=PACK))
+
+
+def parts(ap, count):
+    return ap.rearrange("p (v c) -> p v c", v=count)
 
 
 def tile_picked_layorderegs_none_po_kernel(
@@ -40,8 +51,8 @@ def tile_picked_layorderegs_none_po_kernel(
         keep = ctx.enter_context(tc.tile_pool(name="keep", bufs=1))
         psum = ctx.enter_context(tc.psum_pool(name="psum", bufs=1))
 
-        def tile(name, shape, dtype, tag=""):
-            return keep.tile(shape, dtype, name=name, tag=tag or name, align_bytes=64)
+        def tile(name, shape, dtype, after=""):
+            return keep.tile(shape, dtype, name=name, tag=after or name, align_bytes=64)
 
         offs_sb = tile("offs_sb", [P, S // LANES], U16)
         n1_sb = tile("n1_sb", [P, W // LANES], U16)
@@ -62,20 +73,17 @@ def tile_picked_layorderegs_none_po_kernel(
 
         nc.sync.dma_start(offs_sb[:], offs)
         nc.sync.dma_start(out=xw[:], in_=x_words[0].rearrange("p n t -> p (n t)").bitcast(I32))
-        load_scale_rows(nc.scalar, xs[:], x_scales[0], range(4))
-        load_scale_rows(nc.scalar, w1s_raw[:], w1_scales[0], range(2))
-        load_scale_rows(nc.gpsimd, w1s_raw[:], w1_scales[0], range(2, 4))
+        load_scale_rows(nc.scalar, xs[:], x_scales[0], range(QUADRANTS))
+        load_scale_rows(nc.scalar, w1s_raw[:], w1_scales[0], range(QUADRANTS // 2))
+        load_scale_rows(nc.gpsimd, w1s_raw[:], w1_scales[0], range(QUADRANTS // 2, QUADRANTS))
         nc.sync.dma_start(out=w1w_raw[:].bitcast(I32), in_=w1_words[0].bitcast(I32))
         nc.sync.dma_start(n1_sb[:], n1)
         nc.sync.dma_start(n2_sb[:], n2)
-        load_scale_rows(nc.sync, w2s_raw[:], w2_scales[0], range(4))
+        load_scale_rows(nc.sync, w2s_raw[:], w2_scales[0], range(QUADRANTS))
         nc.sync.dma_start(out=w2w_raw[:].bitcast(I32), in_=w2_words[0].bitcast(I32))
         nc.sync.dma_start(out=gn_sb[:], in_=gn.rearrange("(p t) o -> p (t o)", t=PACK))
         nc.sync.dma_start(out=tau_sb[:], in_=tau.rearrange("(p t) o -> p (t o)", t=PACK))
         nc.sync.dma_start(n3_sb[:], n3)
-
-        def deal(engine_copy, dealt, raw):
-            engine_copy(out=dealt.rearrange("p (t m) -> p t m", t=PACK), in_=raw.rearrange("p (m t) -> p t m", t=PACK))
 
         w1w = tile("w1w", [P, 2 * H], U8)
         w1s = tile("w1s", [P, H], U8)
@@ -106,9 +114,9 @@ def tile_picked_layorderegs_none_po_kernel(
             return banks
 
         y_banks = product("y_bank", w1w, w1s, xw_pick, xs_pick)
-        w2s = tile("w2s", [P, N], U8, tag="w1s_raw")
+        w2s = tile("w2s", [P, N], U8, after="w1s_raw")
         deal(nc.gpsimd.tensor_copy, w2s[:], w2s_raw[:])
-        ident = tile("ident", [P, P], F32, tag="w2s_raw")
+        ident = tile("ident", [P, P], F32, after="w2s_raw")
         make_identity(nc, ident[:])
 
         rows = [tile(f"rows{t}", [P, 2 * S], F32) for t in range(PACK)]
@@ -125,45 +133,34 @@ def tile_picked_layorderegs_none_po_kernel(
         def scalar_move(out, in_):
             nc.scalar.activation(out, in_, ACT.Copy)
 
+        vector_move = nc.vector.tensor_copy
+
         def fetch(t, plain, move_a, move_b):
             plain(y[t], y_banks[t][:])
             move_a(pa[t][:], y[t].indirect(n1_sb[:]))
             move_b(pb[t][:], y[t].indirect(n2_sb[:]))
 
-        def order(t):
-            nc.vector.tensor_tensor(ra[t][:], pa[t][:], pb[t][:], ALU.max)
-            nc.vector.tensor_tensor(rb[t][:], pa[t][:], pb[t][:], ALU.min)
-
-        def put_larger(t, move):
-            move(dt[t][:].indirect(n1_sb[:]), ra[t][:])
-
-        def put_smaller(t, move):
-            move(dt[t][:].indirect(n2_sb[:]), rb[t][:])
-
-        def gain(t):
-            engine = nc.gpsimd if t < 2 else nc.vector
-            engine.tensor_scalar(z_pairs[:, t // 2, :, t % 2], dt[t][:], gn_sb[:, t : t + 1], 0.0, ALU.mult, ALU.add)
-
-        vector_move = nc.vector.tensor_copy
         fetch(0, nc.scalar.copy, scalar_move, scalar_move)
         fetch(1, vector_move, vector_move, vector_move)
         fetch(2, nc.scalar.copy, scalar_move, scalar_move)
         fetch(3, nc.scalar.copy, scalar_move, vector_move)
         for t in range(PACK):
-            order(t)
+            nc.vector.tensor_tensor(ra[t][:], pa[t][:], pb[t][:], ALU.max)
+            nc.vector.tensor_tensor(rb[t][:], pa[t][:], pb[t][:], ALU.min)
         for t in range(PACK):
-            move = scalar_move if t < 2 else vector_move
-            put_larger(t, move)
-            put_smaller(t, move)
+            move = scalar_move if t < PACK // 2 else vector_move
+            move(dt[t][:].indirect(n1_sb[:]), ra[t][:])
+            move(dt[t][:].indirect(n2_sb[:]), rb[t][:])
         for t in (2, 0, 3, 1):
-            gain(t)
+            engine = nc.gpsimd if t < PACK // 2 else nc.vector
+            engine.tensor_scalar(z_pairs[:, t // 2, :, t % 2], dt[t][:], gn_sb[:, t : t + 1], 0.0, ALU.mult, ALU.add)
 
         z_codes = tile("z_codes", [P, S], U32)
         z_scales = tile("z_scales", [P, S], U8)
         pair_words = z_pairs[:].rearrange("p u c e -> p u (c e)").bitcast(F32).rearrange("p u c -> p c u")
         z_words = z_bf[:].rearrange("p c t -> p (c t)").bitcast(F32).rearrange("p (c u) -> p c u", u=2)
-        nc.vector.tensor_copy(z_words[:, :HALF, :], pair_words[:, :HALF, :])
-        nc.scalar.copy(z_words[:, HALF:, :], pair_words[:, HALF:, :])
+        for lo in (0, HALF):
+            nc.vector.tensor_copy(z_words[:, lo : lo + HALF, :], pair_words[:, lo : lo + HALF, :])
         for lo in (0, HALF):
             nc.vector.quantize_mx(
                 out=z_codes[:, lo : lo + HALF].bitcast(FP8X4),
@@ -179,42 +176,36 @@ def tile_picked_layorderegs_none_po_kernel(
             nc.vector.tensor_scalar(shift[t][:], top[t][:], tau_sb[:, t : t + 1], -1.0, ALU.mult, ALU.mult)
 
         out_rows = out_0.rearrange("(p t) c -> p t c", t=PACK)
-        res = tile("res", [P, PACK * S], F32)
-
-        mid, quarter = HALF // 2, HALF // 4
-        units = [(i % PACK, i // PACK * HALF) for i in range(2 * PACK)]
+        res = parts(tile("res", [P, PACK * S], F32)[:], PACK)
 
         members = []
-        for i, (t, lo) in enumerate(units):
+        for i, (t, lo) in enumerate(UNITS):
             ea = tile(f"ea{i}", [P, HALF * MEMBERS], F32)
             members.append(ea[:].rearrange("p (c e) -> p c e", e=MEMBERS))
-            for c in range(0, HALF, PIECE):
+            for c in range(0, HALF, BLOCK):
                 nc.scalar.activation(
-                    ea[:, c * MEMBERS : (c + PIECE) * MEMBERS],
-                    rows[t][:].indirect(n3_sb[:, (lo + c) * MEMBERS // LANES : (lo + c + PIECE) * MEMBERS // LANES]),
+                    ea[:, c * MEMBERS : (c + BLOCK) * MEMBERS],
+                    rows[t][:].indirect(n3_sb[:, (lo + c) * MEMBERS // LANES : (lo + c + BLOCK) * MEMBERS // LANES]),
                     ACT.Exp,
                     bias=shift[t][:],
                     scale=tau_sb[:, t : t + 1],
                 )
 
-        def parts(ap, count):
-            return ap.rearrange("p (v c) -> p v c", v=count)
-
         def turn_and_add(i, u):
-            bank = y_banks[2 + i % 2 if u else 0][:, :mid]
+            sums = y_banks[2 + i % 2 if u else 0][:, :BLOCK]
             for e in range(MEMBERS):
                 nc.tensor.matmul(
-                    bank,
-                    members[i][:, u * mid : (u + 1) * mid, e],
+                    sums,
+                    members[i][:, u * BLOCK : (u + 1) * BLOCK, e],
                     ident[:],
                     is_transpose=True,
                     start=(e == 0),
                     stop=(e == MEMBERS - 1),
                 )
-            return bank
+            return sums
 
         def add_halves(i, half, u):
-            block = members[i][:, u * mid : (u + 1) * mid, :]
+            block = members[i][:, u * BLOCK : (u + 1) * BLOCK, :]
             nc.vector.tensor_tensor(half[:, u, :, :], block[:, :, 0:2], block[:, :, 2:4], ALU.add)
 
         def add_up(half, den, u):
@@ -222,41 +213,37 @@ def tile_picked_layorderegs_none_po_kernel(
 
         def begin(i):
             if i in VECTOR_UNITS:
-                half = tile(f"half{i}", [P, 2, mid, 2], F32, tag=f"whole{i - 1}")
+                half = tile(f"half{i}", [P, 2, BLOCK, 2], F32, after=f"whole{i - 1}")
                 add_halves(i, half, 0)
                 return half
-            early = tile(f"early{i}", [P, mid], F32, tag=f"whole{i - 1}")
+            early = tile(f"early{i}", [P, BLOCK], F32, after=f"whole{i - 1}")
             nc.vector.tensor_scalar(early[:], turn_and_add(i, 0), 0.5, None, ALU.add)
             return early
 
         def store(i):
-            t, lo = units[i]
-            nc.sync.dma_start(out=out_rows[:, t, lo : lo + HALF], in_=res[:, t * S + lo : t * S + lo + HALF])
+            t, lo = UNITS[i]
+            nc.sync.dma_start(out=out_rows[:, t, lo : lo + HALF], in_=res[:, t, lo : lo + HALF])
 
         def finish(i):
             if i < 0 or i in VECTOR_UNITS:
                 return
-            t, lo = units[i]
+            t, lo = UNITS[i]
+            back = y_banks[2 + i % 2][:, BLOCK : BLOCK + HALF]
             nc.vector.scalar_tensor_tensor(
-                res[:, t * S + lo : t * S + lo + HALF],
-                h[t][:, lo : lo + HALF],
-                1.5,
-                y_banks[2 + i % 2][:, mid : mid + HALF],
-                ALU.mult,
-                ALU.mult,
+                res[:, t, lo : lo + HALF], h[t][:, lo : lo + HALF], 1.5, back, ALU.mult, ALU.mult
             )
             store(i)
 
         begun = begin(0)
-        for i, (t, lo) in enumerate(units):
-            pair = tile(f"pair{i}", [P, mid], F32)
+        for i, (t, lo) in enumerate(UNITS):
+            pair = tile(f"pair{i}", [P, BLOCK], F32)
             pair_swapped = parts(pair[:], 2)[:, ::-1, :]
-            whole = tile(f"whole{i}", [P, quarter], F32)
-            inv = tile(f"inv{i}", [P, quarter], F32)
-            inv_all = inv[:].unsqueeze(1).to_broadcast([P, 4, quarter])
+            whole = tile(f"whole{i}", [P, QUARTER], F32)
+            inv = tile(f"inv{i}", [P, QUARTER], F32)
+            inv_all = inv[:].unsqueeze(1).to_broadcast([P, 4, QUARTER])
             others = tile(f"others{i}", [P, HALF], F32)
             if i in VECTOR_UNITS:
-                den = tile(f"den{i}", [P, 2, mid], F32)
+                den = tile(f"den{i}", [P, 2, BLOCK], F32)
                 num = tile(f"num{i}", [P, HALF], F32)
                 add_up(begun, den, 0)
                 add_halves(i, begun, 1)
@@ -266,42 +253,45 @@ def tile_picked_layorderegs_none_po_kernel(
                 nc.vector.scalar_tensor_tensor(
                     parts(num[:], 2), parts(h[t][:, lo : lo + HALF], 2), 1.5, den[:, ::-1, :], ALU.mult, ALU.mult
                 )
-                nc.vector.tensor_tensor(whole[:], pair[:, :quarter], pair[:, quarter:], ALU.mult)
+                nc.vector.tensor_tensor(whole[:], pair[:, :QUARTER], pair[:, QUARTER:], ALU.mult)
                 nc.vector.tensor_tensor(
                     others[:].rearrange("p (u v c) -> p u v c", u=2, v=2),
                     num[:].rearrange("p (u v c) -> p u v c", u=2, v=2),
-                    pair_swapped.unsqueeze(1).to_broadcast([P, 2, 2, quarter]),
+                    pair_swapped.unsqueeze(1).to_broadcast([P, 2, 2, QUARTER]),
                     ALU.mult,
                 )
                 nc.vector.reciprocal(inv[:], whole[:])
-                if i + 1 < len(units):
+                if i + 1 < len(UNITS):
                     begun = begin(i + 1)
                 finish(i - 1)
-                nc.vector.tensor_tensor(
-                    parts(res[:, t * S + lo : t * S + lo + HALF], 4), parts(others[:], 4), inv_all, ALU.mult
-                )
+                nc.vector.tensor_tensor(parts(res[:, t, lo : lo + HALF], 4), parts(others[:], 4), inv_all, ALU.mult)
                 store(i)
                 continue
             early, late = begun, turn_and_add(i, 1)
             recip = tile(f"recip{i}", [P, HALF], F32)
             nc.vector.scalar_tensor_tensor(pair[:], late, 0.5, early[:], ALU.add, ALU.mult)
             finish(i - 2)
-            nc.vector.tensor_tensor(whole[:], pair[:, :quarter], pair[:, quarter:], ALU.mult)
-            nc.gpsimd.tensor_tensor(parts(others[:, mid:], 2), parts(early[:], 2), pair_swapped, ALU.mult)
-            nc.vector.scalar_tensor_tensor(parts(others[:, :mid], 2), parts(late, 2), 0.5, pair_swapped, ALU.add, ALU.mult)
+            nc.vector.tensor_tensor(whole[:], pair[:, :QUARTER], pair[:, QUARTER:], ALU.mult)
+            nc.gpsimd.tensor_tensor(parts(others[:, BLOCK:], 2), parts(early[:], 2), pair_swapped, ALU.mult)
+            nc.vector.scalar_tensor_tensor(
+                parts(others[:, :BLOCK], 2), parts(late, 2), 0.5, pair_swapped, ALU.add, ALU.mult
+            )
             nc.vector.reciprocal(inv[:], whole[:])
-            begun = begin(i + 1)
             engine = nc.vector if i + 1 in VECTOR_UNITS else nc.gpsimd
             engine.tensor_tensor(parts(recip[:], 4), parts(others[:], 4), inv_all, ALU.mult)
             for u in range(2):
-                cols = slice(u * mid, (u + 1) * mid)
-                nc.tensor.transpose(y_banks[2 + i % 2][:, (u + 1) * mid : (u + 2) * mid], recip[:, cols], ident[:])
+                nc.tensor.transpose(
+                    y_banks[2 + i % 2][:, (u + 1) * BLOCK : (u + 2) * BLOCK],
+                    recip[:, u * BLOCK : (u + 1) * BLOCK],
+                    ident[:],
+                )
+            begun = begin(i + 1)
 
-        res_bf = tile("res_bf", [P, S, PACK], BF16, tag=f"shift{PACK - 1}")
-        res_codes = tile("res_codes", [P, S], I32, tag=f"inv{2 * PACK - 1}")
+        res_bf = tile("res_bf", [P, S, PACK], BF16, after=f"shift{PACK - 1}")
+        res_codes = tile("res_codes", [P, S], I32, after=f"inv{len(UNITS) - 1}")
         res_scales = tile("res_scales", [P, S], U8)
         words_out = out_1[0].rearrange("p n t -> p (n t)").bitcast(I32)
-        res_cols = res[:].rearrange("p (t c) -> p c t", t=PACK)
+        res_cols = res.rearrange("p t c -> p c t")
         cut = HALF + SCALAR_LAST
         nc.scalar.copy(out=res_bf[:, :HALF, :], in_=res_cols[:, :HALF, :])
         nc.scalar.copy(out=res_bf[:, HALF:cut, :], in_=res_cols[:, HALF:cut, :])
@@ -314,7 +304,7 @@ def tile_picked_layorderegs_none_po_kernel(
                 in_=res_bf[:, cols, :].rearrange("p c t -> p (c t)"),
             )
             nc.sync.dma_start(out=words_out[:, cols], in_=res_codes[:, cols])
-        for q in range(4):
+        for q in range(QUADRANTS):
             queue = nc.scalar if q % 2 else nc.sync
             queue.dma_start(
                 out=out_2[0].bitcast(I32)[4 * q : 4 * q + 4, :], in_=res_scales[:].bitcast(I32)[32 * q : 32 * q + 4, :]

from contextlib import ExitStack

import concourse.mybir as mybir
from concourse.masks import make_identity

K, T, S, N, H, W, G = 512, 2048, 512, 512, 512, 256, 2048
FLOPS = 2 * K * H * S + 2 * H * N * S

F32 = mybir.dt.float32
BF16 = mybir.dt.bfloat16
I32 = mybir.dt.int32
U32 = mybir.dt.uint32
U16 = mybir.dt.uint16
U8 = mybir.dt.uint8
FP8X4 = mybir.dt.float8_e4m3fn_x4
FP4X4 = mybir.dt.float4_e2m1fn_x4
ALU = mybir.AluOpType
ACT = mybir.ActivationFunctionType

P = 128
PACK = 4
QUADRANTS = 4
MEMBERS = 4
LANES = 16
HALF = S // 2
BLOCK = P
QUARTER = HALF // 4
UNITS = tuple((t, lo) for lo in (0, HALF) for t in range(PACK))
VECTOR_UNITS = (0, len(UNITS) - 1)
SCALAR_LAST = 96


def load_scale_rows(queue, plane, rows, quadrants):
    for q in quadrants:
        queue.dma_start(out=plane.bitcast(I32)[32 * q : 32 * q + 4, :], in_=rows.bitcast(I32)[4 * q : 4 * q + 4, :])


def deal(copy, dealt, raw):
    copy(out=dealt.rearrange("p (t m) -> p t m", t=PACK), in_=raw.rearrange("p (m t) -> p t m", t=PACK))


def parts(ap, count):
    return ap.rearrange("p (v c) -> p v c", v=count)


def tile_picked_layorderegs_none_po_kernel(
    tc, x_words, x_scales, w1_words, w1_scales, gn, w2_words, w2_scales, tau, offs, n1, n2, n3, out_0, out_1, out_2
):
    nc = tc.nc
    with ExitStack() as ctx:
        keep = ctx.enter_context(tc.tile_pool(name="keep", bufs=1))
        psum = ctx.enter_context(tc.psum_pool(name="psum", bufs=1))

        def tile(name, shape, dtype, after=""):
            return keep.tile(shape, dtype, name=name, tag=after or name, align_bytes=64)

        offs_sb = tile("offs_sb", [P, S // LANES], U16)
        n1_sb = tile("n1_sb", [P, W // LANES], U16)
        n2_sb = tile("n2_sb", [P, W // LANES], U16)
        n3_sb = tile("n3_sb", [P, G // LANES], U16)
        xw = tile("xw", [P, T], I32)
        xs = tile("xs", [P, T], U8)
        w1w_raw = tile("w1w_raw", [P, 2 * H], U8)
        w2w_raw = tile("w2w_raw", [P, 2 * N], U8)
        w1s_raw = tile("w1s_raw", [P, H], U8)
        w2s_raw = tile("w2s_raw", [P, N], U8)
        gn_sb = tile("gn_sb", [P, PACK], F32)
        tau_sb = tile("tau_sb", [P, PACK], F32)

        nc.vector.memset(xs[:].bitcast(I32), 0)
        nc.vector.memset(w1s_raw[:].bitcast(I32), 0)
        nc.vector.memset(w2s_raw[:].bitcast(I32), 0)

        nc.sync.dma_start(offs_sb[:], offs)
        nc.sync.dma_start(out=xw[:], in_=x_words[0].rearrange("p n t -> p (n t)").bitcast(I32))
        load_scale_rows(nc.scalar, xs[:], x_scales[0], range(QUADRANTS))
        load_scale_rows(nc.scalar, w1s_raw[:], w1_scales[0], range(QUADRANTS // 2))
        load_scale_rows(nc.gpsimd, w1s_raw[:], w1_scales[0], range(QUADRANTS // 2, QUADRANTS))
        nc.sync.dma_start(out=w1w_raw[:].bitcast(I32), in_=w1_words[0].bitcast(I32))
        nc.sync.dma_start(n1_sb[:], n1)
        nc.sync.dma_start(n2_sb[:], n2)
        load_scale_rows(nc.sync, w2s_raw[:], w2_scales[0], range(QUADRANTS))
        nc.sync.dma_start(out=w2w_raw[:].bitcast(I32), in_=w2_words[0].bitcast(I32))
        nc.sync.dma_start(out=gn_sb[:], in_=gn.rearrange("(p t) o -> p (t o)", t=PACK))
        nc.sync.dma_start(out=tau_sb[:], in_=tau.rearrange("(p t) o -> p (t o)", t=PACK))
        nc.sync.dma_start(n3_sb[:], n3)

        w1w = tile("w1w", [P, 2 * H], U8)
        w1s = tile("w1s", [P, H], U8)
        w2w = tile("w2w", [P, 2 * N], U8)
        deal(nc.scalar.copy, w1w[:].bitcast(U16), w1w_raw[:].bitcast(U16))
        xw_pick = tile("xw_pick", [P, S], U32)
        xs_pick = tile("xs_pick", [P, S], U8)
        nc.vector.tensor_copy(xs_pick[:], xs[:].indirect(offs_sb[:]))
        deal(nc.gpsimd.tensor_copy, w1s[:], w1s_raw[:])
        for lo in (0, HALF):
            entries = offs_sb[:, lo // LANES : (lo + HALF) // LANES]
            nc.vector.tensor_copy(xw_pick[:, lo : lo + HALF], xw[:].bitcast(U32).indirect(entries))
        deal(nc.scalar.copy, w2w[:].bitcast(U16), w2w_raw[:].bitcast(U16))

        def product(name, words, scales, codes, code_scales):
            banks = [psum.tile([P, S], F32, name=f"{name}{t}") for t in range(PACK)]
            for t in range(PACK):
                for lo in (0, HALF):
                    nc.tensor.matmul_mx(
                        out=banks[t][:, lo : lo + HALF],
                        lhsT=words[:, 2 * P * t : 2 * P * (t + 1)].bitcast(FP4X4),
                        lhsT_scale=scales[:, P * t : P * (t + 1)],
                        rhs=codes[:, lo : lo + HALF].bitcast(FP8X4),
                        rhs_scale=code_scales[:, lo : lo + HALF],
                        start=True,
                        stop=True,
                    )
            return banks

        y_banks = product("y_bank", w1w, w1s, xw_pick, xs_pick)
        w2s = tile("w2s", [P, N], U8, after="w1s_raw")
        deal(nc.gpsimd.tensor_copy, w2s[:], w2s_raw[:])
        ident = tile("ident", [P, P], F32, after="w2s_raw")
        make_identity(nc, ident[:])

        rows = [tile(f"rows{t}", [P, 2 * S], F32) for t in range(PACK)]
        y = [rows[t][:, S:] for t in range(PACK)]
        h = [rows[t][:, :S] for t in range(PACK)]
        pa = [tile(f"pa{t}", [P, W], F32) for t in range(PACK)]
        pb = [tile(f"pb{t}", [P, W], F32) for t in range(PACK)]
        ra = [tile(f"ra{t}", [P, W], F32) for t in range(PACK)]
        rb = [tile(f"rb{t}", [P, W], F32) for t in range(PACK)]
        dt = [tile(f"dt{t}", [P, S], F32) for t in range(PACK)]
        z_pairs = tile("z_pairs", [P, 2, S, 2], BF16)
        z_bf = tile("z_bf", [P, S, PACK], BF16)

        def scalar_move(out, in_):
            nc.scalar.activation(out, in_, ACT.Copy)

        vector_move = nc.vector.tensor_copy

        def fetch(t, plain, move_a, move_b):
            plain(y[t], y_banks[t][:])
            move_a(pa[t][:], y[t].indirect(n1_sb[:]))
            move_b(pb[t][:], y[t].indirect(n2_sb[:]))

        fetch(0, nc.scalar.copy, scalar_move, scalar_move)
        fetch(1, vector_move, vector_move, vector_move)
        fetch(2, nc.scalar.copy, scalar_move, scalar_move)
        fetch(3, nc.scalar.copy, scalar_move, vector_move)
        for t in range(PACK):
            nc.vector.tensor_tensor(ra[t][:], pa[t][:], pb[t][:], ALU.max)
            nc.vector.tensor_tensor(rb[t][:], pa[t][:], pb[t][:], ALU.min)
        for t in range(PACK):
            move = scalar_move if t < PACK // 2 else vector_move
            move(dt[t][:].indirect(n1_sb[:]), ra[t][:])
            move(dt[t][:].indirect(n2_sb[:]), rb[t][:])
        for t in (2, 0, 3, 1):
            engine = nc.gpsimd if t < PACK // 2 else nc.vector
            engine.tensor_scalar(z_pairs[:, t // 2, :, t % 2], dt[t][:], gn_sb[:, t : t + 1], 0.0, ALU.mult, ALU.add)

        z_codes = tile("z_codes", [P, S], U32)
        z_scales = tile("z_scales", [P, S], U8)
        pair_words = z_pairs[:].rearrange("p u c e -> p u (c e)").bitcast(F32).rearrange("p u c -> p c u")
        z_words = z_bf[:].rearrange("p c t -> p (c t)").bitcast(F32).rearrange("p (c u) -> p c u", u=2)
        for lo in (0, HALF):
            nc.vector.tensor_copy(z_words[:, lo : lo + HALF, :], pair_words[:, lo : lo + HALF, :])
        for lo in (0, HALF):
            nc.vector.quantize_mx(
                out=z_codes[:, lo : lo + HALF].bitcast(FP8X4),
                scales=z_scales[:, lo : lo + HALF],
                in_=z_bf[:, lo : lo + HALF, :].rearrange("p c t -> p (c t)"),
            )
        h_banks = product("h_bank", w2w, w2s, z_codes, z_scales)

        top = [tile(f"top{t}", [P, 1], F32) for t in range(PACK)]
        shift = [tile(f"shift{t}", [P, 1], F32) for t in range(PACK)]
        for t in range(PACK):
            nc.vector.tensor_scalar(h[t], h_banks[t][:], 1.0, None, ALU.mult, ALU.max, accum_out=top[t][:])
            nc.vector.tensor_scalar(shift[t][:], top[t][:], tau_sb[:, t : t + 1], -1.0, ALU.mult, ALU.mult)

        out_rows = out_0.rearrange("(p t) c -> p t c", t=PACK)
        res = parts(tile("res", [P, PACK * S], F32)[:], PACK)

        members = []
        for i, (t, lo) in enumerate(UNITS):
            ea = tile(f"ea{i}", [P, HALF * MEMBERS], F32)
            members.append(ea[:].rearrange("p (c e) -> p c e", e=MEMBERS))
            for c in range(0, HALF, BLOCK):
                nc.scalar.activation(
                    ea[:, c * MEMBERS : (c + BLOCK) * MEMBERS],
                    rows[t][:].indirect(n3_sb[:, (lo + c) * MEMBERS // LANES : (lo + c + BLOCK) * MEMBERS // LANES]),
                    ACT.Exp,
                    bias=shift[t][:],
                    scale=tau_sb[:, t : t + 1],
                )

        def turn_and_add(i, u):
            sums = y_banks[2 + i % 2 if u else 0][:, :BLOCK]
            for e in range(MEMBERS):
                nc.tensor.matmul(
                    sums,
                    members[i][:, u * BLOCK : (u + 1) * BLOCK, e],
                    ident[:],
                    is_transpose=True,
                    start=(e == 0),
                    stop=(e == MEMBERS - 1),
                )
            return sums

        def add_halves(i, half, u):
            block = members[i][:, u * BLOCK : (u + 1) * BLOCK, :]
            nc.vector.tensor_tensor(half[:, u, :, :], block[:, :, 0:2], block[:, :, 2:4], ALU.add)

        def add_up(half, den, u):
            nc.vector.scalar_tensor_tensor(den[:, u, :], half[:, u, :, 0], 0.5, half[:, u, :, 1], ALU.add, ALU.add)

        def begin(i):
            if i in VECTOR_UNITS:
                half = tile(f"half{i}", [P, 2, BLOCK, 2], F32, after=f"whole{i - 1}")
                add_halves(i, half, 0)
                return half
            early = tile(f"early{i}", [P, BLOCK], F32, after=f"whole{i - 1}")
            nc.vector.tensor_scalar(early[:], turn_and_add(i, 0), 0.5, None, ALU.add)
            return early

        def store(i):
            t, lo = UNITS[i]
            nc.sync.dma_start(out=out_rows[:, t, lo : lo + HALF], in_=res[:, t, lo : lo + HALF])

        def finish(i):
            if i < 0 or i in VECTOR_UNITS:
                return
            t, lo = UNITS[i]
            back = y_banks[2 + i % 2][:, BLOCK : BLOCK + HALF]
            nc.vector.scalar_tensor_tensor(
                res[:, t, lo : lo + HALF], h[t][:, lo : lo + HALF], 1.5, back, ALU.mult, ALU.mult
            )
            store(i)

        begun = begin(0)
        for i, (t, lo) in enumerate(UNITS):
            pair = tile(f"pair{i}", [P, BLOCK], F32)
            pair_swapped = parts(pair[:], 2)[:, ::-1, :]
            whole = tile(f"whole{i}", [P, QUARTER], F32)
            inv = tile(f"inv{i}", [P, QUARTER], F32)
            inv_all = inv[:].unsqueeze(1).to_broadcast([P, 4, QUARTER])
            others = tile(f"others{i}", [P, HALF], F32)
            if i in VECTOR_UNITS:
                den = tile(f"den{i}", [P, 2, BLOCK], F32)
                num = tile(f"num{i}", [P, HALF], F32)
                add_up(begun, den, 0)
                add_halves(i, begun, 1)
                finish(i - 2)
                add_up(begun, den, 1)
                nc.vector.tensor_tensor(pair[:], den[:, 0, :], den[:, 1, :], ALU.mult)
                nc.vector.scalar_tensor_tensor(
                    parts(num[:], 2), parts(h[t][:, lo : lo + HALF], 2), 1.5, den[:, ::-1, :], ALU.mult, ALU.mult
                )
                nc.vector.tensor_tensor(whole[:], pair[:, :QUARTER], pair[:, QUARTER:], ALU.mult)
                nc.vector.tensor_tensor(
                    others[:].rearrange("p (u v c) -> p u v c", u=2, v=2),
                    num[:].rearrange("p (u v c) -> p u v c", u=2, v=2),
                    pair_swapped.unsqueeze(1).to_broadcast([P, 2, 2, QUARTER]),
                    ALU.mult,
                )
                nc.vector.reciprocal(inv[:], whole[:])
                if i + 1 < len(UNITS):
                    begun = begin(i + 1)
                finish(i - 1)
                nc.vector.tensor_tensor(parts(res[:, t, lo : lo + HALF], 4), parts(others[:], 4), inv_all, ALU.mult)
                store(i)
                continue
            early, late = begun, turn_and_add(i, 1)
            recip = tile(f"recip{i}", [P, HALF], F32)
            nc.vector.scalar_tensor_tensor(pair[:], late, 0.5, early[:], ALU.add, ALU.mult)
            finish(i - 2)
            nc.vector.tensor_tensor(whole[:], pair[:, :QUARTER], pair[:, QUARTER:], ALU.mult)
            nc.gpsimd.tensor_tensor(parts(others[:, BLOCK:], 2), parts(early[:], 2), pair_swapped, ALU.mult)
            nc.vector.scalar_tensor_tensor(
                parts(others[:, :BLOCK], 2), parts(late, 2), 0.5, pair_swapped, ALU.add, ALU.mult
            )
            nc.vector.reciprocal(inv[:], whole[:])
            engine = nc.vector if i + 1 in VECTOR_UNITS else nc.gpsimd
            engine.tensor_tensor(parts(recip[:], 4), parts(others[:], 4), inv_all, ALU.mult)
            for u in range(2):
                nc.tensor.transpose(
                    y_banks[2 + i % 2][:, (u + 1) * BLOCK : (u + 2) * BLOCK],
                    recip[:, u * BLOCK : (u + 1) * BLOCK],
                    ident[:],
                )
            begun = begin(i + 1)

        res_bf = tile("res_bf", [P, S, PACK], BF16, after=f"shift{PACK - 1}")
        res_codes = tile("res_codes", [P, S], I32, after=f"inv{len(UNITS) - 1}")
        res_scales = tile("res_scales", [P, S], U8)
        words_out = out_1[0].rearrange("p n t -> p (n t)").bitcast(I32)
        res_cols = res.rearrange("p t c -> p c t")
        cut = HALF + SCALAR_LAST
        nc.scalar.copy(out=res_bf[:, :HALF, :], in_=res_cols[:, :HALF, :])
        nc.scalar.copy(out=res_bf[:, HALF:cut, :], in_=res_cols[:, HALF:cut, :])
        nc.vector.tensor_copy(out=res_bf[:, cut:, :], in_=res_cols[:, cut:, :])
        for lo in (0, HALF):
            cols = slice(lo, lo + HALF)
            nc.vector.quantize_mx(
                out=res_codes[:, cols].bitcast(FP8X4),
                scales=res_scales[:, cols],
                in_=res_bf[:, cols, :].rearrange("p c t -> p (c t)"),
            )
            nc.sync.dma_start(out=words_out[:, cols], in_=res_codes[:, cols])
        for q in range(QUADRANTS):
            queue = nc.scalar if q % 2 else nc.sync
            queue.dma_start(
                out=out_2[0].bitcast(I32)[4 * q : 4 * q + 4, :], in_=res_scales[:].bitcast(I32)[32 * q : 32 * q + 4, :]
            )
